import numpy as np
import ml_dtypes


def mxq(x, axis, fmt="e4m3"):
    dtype, down = {"e4m3": (ml_dtypes.float8_e4m3fn, 7), "e5m2": (ml_dtypes.float8_e5m2, 14)}[fmt]
    v = np.moveaxis(np.asarray(x, np.float32).astype(ml_dtypes.bfloat16).astype(np.float64), axis, -1)
    blocks = v.reshape(v.shape[:-1] + (-1, 32))
    amax = np.abs(blocks).max(-1, keepdims=True)
    byte = np.maximum(np.where(amax > 0, np.frexp(amax)[1] - 1 + 127, 0) - down, 1)
    scale = np.exp2(byte - 127.0)
    codes = (blocks / scale).astype(np.float32).astype(dtype).astype(np.float64)
    return np.moveaxis((codes * scale).reshape(v.shape), -1, axis)


WIDE = False


def mx_kscale(k):
    if not WIDE:
        return np.ones(k)
    levels = np.array([10, -10, 5, -5, 0])
    if k % 512:
        return np.exp2(np.random.permutation(np.resize(levels, k // 32))).repeat(32)
    a = np.empty((k // 512, 16))
    for p in range(k // 512):
        a[p, :8] = np.random.permutation(np.resize(levels, 8))
        for g in range(8):
            far = levels[np.abs(levels - a[p, g]) >= 10]
            a[p, g + 8] = far[np.random.randint(len(far))]
    return np.exp2(a.ravel()).repeat(32)


def f64(x):
    return np.asarray(x).astype(np.float64)


def striped(idx):
    return np.tile(np.asarray(idx).reshape(-1, 16).T, (8, 1)).astype(np.uint16)


def unstriped(offs):
    return offs[:16].T.reshape(-1).astype(np.int64)


E2M1 = np.array([0.0, 0.5, 1.0, 1.5, 2.0, 3.0, 4.0, 6.0, -0.0, -0.5, -1.0, -1.5, -2.0, -3.0, -4.0, -6.0])


def pack_weight(w, fmt):
    k, n = w.shape
    w = f64(np.asarray(w, np.float32).astype(ml_dtypes.bfloat16)).reshape(k // 32, 32, n)
    amax = np.abs(w).max(1)
    if fmt == "e4m3":
        byte = np.frexp(amax)[1] - 1 + 127 - 7
    else:
        mant, ex = np.frexp(amax / 6.0)
        byte = np.where(mant > 0.5, ex, ex - 1) + 127
    byte = np.clip(np.where(amax > 0, byte, 1), 1, 254)
    scaled = (w * np.exp2(127.0 - byte)[:, None, :]).reshape(k, n).astype(np.float32)
    by_word = np.ascontiguousarray(scaled.reshape(k // 512, 128, 4, n).transpose(0, 1, 3, 2))
    if fmt == "e4m3":
        words = by_word.astype(ml_dtypes.float8_e4m3fn).view(np.uint8)
    else:
        c = by_word.astype(ml_dtypes.float4_e2m1fn).view(np.uint8) & 0xF
        words = (c[..., 0::2] | (c[..., 1::2] << 4)).reshape(k // 512, 128, 2 * n)
    return np.ascontiguousarray(words), np.ascontiguousarray(byte.astype(np.uint8).reshape(k // 512, 16, n))


def unpack_weight(words, scales, fmt):
    g, _, n = scales.shape
    words = np.ascontiguousarray(words).reshape(g, 128, n, -1)
    if fmt == "e4m3":
        vals = words.view(ml_dtypes.float8_e4m3fn).astype(np.float64)
    else:
        nib = np.empty((g, 128, n, 4), np.uint8)
        nib[..., 0::2] = words & 0xF
        nib[..., 1::2] = words >> 4
        vals = E2M1[nib]
    vals = vals * np.repeat(np.exp2(scales.astype(np.float64) - 127.0), 8, axis=1)[..., None]
    return vals.transpose(0, 1, 3, 2).reshape(g * 512, n)


K, J, T, R, N = 2048, 512, 512, 512, 512


def setup_inputs():
    n = np.random.standard_normal
    idx = np.random.permutation(K)[:J]
    fk = mx_kscale(K)
    fr = mx_kscale(R)
    fj = mx_kscale(J)
    tj = np.ones(K)
    tj[idx] = fj
    xo = n((T, K))
    xo[:, idx] *= 3.0
    xr = xo.copy()
    xr[:, idx] = 0.0
    xbp = pack_weight(xr.T / fk[:, None], "e2m1")
    wbp = pack_weight(n((K, R)) * 1 / np.sqrt(K) * fk[:, None] * fr, "e2m1")
    wop = pack_weight(n((J, R)) * 1 / np.sqrt(J) * fj[:, None] * fr, "e4m3")
    return {
        "xb_words": xbp[0],
        "xb_scales": xbp[1],
        "wb_words": wbp[0],
        "wb_scales": wbp[1],
        "xt": (xo / tj).astype(np.float32),
        "wo_words": wop[0],
        "wo_scales": wop[1],
        "wd": (n((R, N)) * 1 / np.sqrt(R) / fr[:, None]).astype(np.float32),
        "offs": striped(idx),
    }


def reference(xb_words, xb_scales, wb_words, wb_scales, xt, wo_words, wo_scales, wd, offs):
    idx = unstriped(offs)
    xbu = unpack_weight(xb_words, xb_scales, "e2m1")
    wbu = unpack_weight(wb_words, wb_scales, "e2m1")
    wou = unpack_weight(wo_words, wo_scales, "e4m3")
    xo = f64(xt)[:, idx].T
    xoq = mxq(xo, 0, "e4m3")
    z = wbu.T @ xbu + wou.T @ xoq
    hid = np.maximum(z, 0.0)
    wdq = mxq(f64(wd), 0, "e4m3")
    hidq = mxq(hid, 0, "e4m3")
    y = wdq.T @ hidq
    return y

@@ -1,0 +1,196 @@
+from contextlib import ExitStack
+
+import concourse.mybir as mybir
+from concourse.masks import make_identity
+
+K, J, T, R, N = 2048, 512, 512, 512, 512
+FLOPS = 2 * T * R * (K + J) + 2 * T * R * N
+
+F32 = mybir.dt.float32
+BF16 = mybir.dt.bfloat16
+I32 = mybir.dt.int32
+U32 = mybir.dt.uint32
+U16 = mybir.dt.uint16
+U8 = mybir.dt.uint8
+FP8X4 = mybir.dt.float8_e4m3fn_x4
+FP4X4 = mybir.dt.float4_e2m1fn_x4
+RELU = mybir.ActivationFunctionType.Relu
+
+P = 128
+PACK = 4
+PASSES = K // (P * PACK)
+TILES = T // P
+
+
+def load_scale_rows(queue, plane, scales):
+    for r in range(4):
+        queue.dma_start(
+            out=plane[r:P:32, :, :].bitcast(I32),
+            in_=scales[:, r:16:4, :].rearrange("z q c -> q z c").bitcast(I32),
+        )
+
+
+def tile_list_outlier_channels_mlp_kernel(
+    tc, xb_words, xb_scales, wb_words, wb_scales, xt, wo_words, wo_scales, wd, offs, out
+):
+    nc = tc.nc
+    with ExitStack() as ctx:
+        keep = ctx.enter_context(tc.tile_pool(name="keep", bufs=1))
+        work = ctx.enter_context(tc.tile_pool(name="work", bufs=2))
+        z_psum = ctx.enter_context(tc.psum_pool(name="z_psum", bufs=2))
+        turn_psum = ctx.enter_context(tc.psum_pool(name="turn_psum", bufs=2))
+        y_psum = ctx.enter_context(tc.psum_pool(name="y_psum", bufs=4))
+
+        offsets = keep.tile([P, J // 16], U16, name="offsets")
+        wb_scale_raw = keep.tile([P, PASSES, R], U8, align_bytes=64)
+        wb_scale = keep.tile([P, PASSES, PACK, P], U8, align_bytes=64)
+        xb_scale = keep.tile([P, PASSES, T], U8, align_bytes=64)
+        wo_scale_raw = keep.tile([P, 1, R], U8, align_bytes=64)
+        nc.gpsimd.memset(xb_scale[:].bitcast(I32), 0)
+        nc.vector.memset(wo_scale_raw[:].bitcast(I32), 0)
+        identity = keep.tile([P, P], F32)
+        nc.vector.memset(identity[:], 0.0)
+        make_identity(nc, identity[:], nomemset=True)
+        nc.vector.memset(wb_scale[:].bitcast(I32), 0)
+
+        for q in range(4):
+            nc.scalar.dma_start(
+                out=wb_scale_raw[32 * q : 32 * q + 4, :, :].bitcast(I32),
+                in_=wb_scales[:, 4 * q : 4 * q + 4, :].rearrange("z r c -> r z c").bitcast(I32),
+            )
+        load_scale_rows(nc.scalar, xb_scale, xb_scales)
+        load_scale_rows(nc.gpsimd, wo_scale_raw, wo_scales)
+
+        wb_raw = keep.tile([P, PASSES, 2 * R], U8, align_bytes=64)
+        xb = keep.tile([P, PASSES, 2 * T], U8, align_bytes=64)
+        wo_raw = keep.tile([P, R], I32, align_bytes=64)
+        nc.sync.dma_start(out=wb_raw[:].bitcast(I32), in_=wb_words.rearrange("z p c -> p z c").bitcast(I32))
+        nc.sync.dma_start(out=xb[:].bitcast(I32), in_=xb_words.rearrange("z p c -> p z c").bitcast(I32))
+        nc.sync.dma_start(offsets[:], offs)
+        nc.sync.dma_start(out=wo_raw[:], in_=wo_words[0].rearrange("p c t -> p (c t)").bitcast(I32))
+        rows = [keep.tile([P, K], F32, name=f"rows{i}") for i in range(TILES)]
+        for i in range(TILES):
+            nc.sync.dma_start(out=rows[i][:], in_=xt[i * P : (i + 1) * P, :])
+        wd_raw = keep.tile([P, PACK, N], F32)
+        wd_rows = wd.rearrange("(m j e) n -> e m j n", j=PACK, e=4)
+        for e in range(4):
+            nc.sync.dma_start(out=wd_raw[e:P:4, :, :], in_=wd_rows[e])
+
+        wb = keep.tile([P, PASSES, PACK, 2 * P], U8, align_bytes=64)
+        wo = keep.tile([P, PACK, P], I32, align_bytes=64)
+        wo_scale = keep.tile([P, PACK, P], U8, align_bytes=64)
+        nc.vector.tensor_copy(
+            out=wb[:].bitcast(I32).rearrange("p z j (m w) -> p z j m w", w=2),
+            in_=wb_raw[:].bitcast(I32).rearrange("p z (m j w) -> p z j m w", j=PACK, w=2),
+        )
+        for q in range(4):
+            live = slice(32 * q, 32 * q + 4)
+            nc.vector.tensor_copy(
+                out=wb_scale[live].bitcast(I32),
+                in_=wb_scale_raw[live].bitcast(I32).rearrange("p z (m j) -> p z j m", j=PACK),
+            )
+        nc.vector.tensor_copy(
+            out=wo[:].rearrange("p j (m e) -> p j m e", e=4),
+            in_=wo_raw[:].rearrange("p (m j e) -> p j m e", j=PACK, e=4),
+        )
+        nc.vector.tensor_copy(
+            out=wo_scale[:].bitcast(I32),
+            in_=wo_scale_raw[:, 0, :].bitcast(I32).rearrange("p (m j) -> p j m", j=PACK),
+        )
+
+        hid_codes = keep.tile([P, T], U32, align_bytes=64)
+        hid_scale = keep.tile([P, T], U8, align_bytes=64)
+        for i in range(TILES):
+            tokens = slice(i * P, (i + 1) * P)
+            z = z_psum.tile([P, PACK, P], F32)
+            for j in range(PACK):
+                for g in range(PASSES):
+                    nc.tensor.matmul_mx(
+                        out=z[:, j, :],
+                        lhsT=wb[:, g, j, :].bitcast(FP4X4),
+                        lhsT_scale=wb_scale[:, g, j, :],
+                        rhs=xb[:, g, 2 * i * P : 2 * (i + 1) * P].bitcast(FP4X4),
+                        rhs_scale=xb_scale[:, g, tokens],
+                        start=(j == 0 and g == 0),
+                        stop=False,
+                    )
+            picked = work.tile([P, J], BF16, align_bytes=64)
+            nc.vector.tensor_copy(out=picked[:], in_=rows[i][:].indirect(offsets[:]))
+            turned = turn_psum.tile([P, 2, P], F32)
+            pairs = picked[:].bitcast(F32)
+            for u in range(2):
+                nc.tensor.transpose(turned[:, u, :], pairs[:, u : J // 2 : 2], identity[:])
+            xo = work.tile([P, P * PACK], BF16, align_bytes=64)
+            nc.scalar.copy(
+                out=xo[:].bitcast(F32).rearrange("p (t u) -> p t u", u=2),
+                in_=turned[:].rearrange("p u t -> p t u"),
+            )
+            xo_codes = work.tile([P, P], U32, align_bytes=64)
+            xo_scale = work.tile([P, P], U8, align_bytes=64)
+            nc.vector.quantize_mx(out=xo_codes[:].bitcast(FP8X4), scales=xo_scale[:], in_=xo[:])
+            for j in range(PACK):
+                nc.tensor.matmul_mx(
+                    out=z[:, j, :],
+                    lhsT=wo[:, j, :].bitcast(FP8X4),
+                    lhsT_scale=wo_scale[:, j, :],
+                    rhs=xo_codes[:].bitcast(FP8X4),
+                    rhs_scale=xo_scale[:],
+                    start=False,
+                    stop=(j == PACK - 1),
+                )
+            hid = work.tile([P, P * PACK], BF16, align_bytes=64)
+            nc.scalar.activation(
+                out=hid[:].rearrange("p (t j) -> p t j", j=PACK),
+                in_=z[:].rearrange("p j t -> p t j"),
+                func=RELU,
+            )
+            nc.vector.quantize_mx(out=hid_codes[:, tokens].bitcast(FP8X4), scales=hid_scale[:, tokens], in_=hid[:])
+
+        wd_codes = keep.tile([P, N], U32, align_bytes=64)
+        wd_scale = keep.tile([P, N], U8, align_bytes=64)
+        last = slice(T - P, T)
+        for h in range(2):
+            cols = slice(h * 256, (h + 1) * 256)
+            wd_bf = work.tile([P, 256 * PACK], BF16, align_bytes=64)
+            nc.vector.tensor_copy(
+                out=wd_bf[:].rearrange("p (c i j) -> p c j i", i=4, j=PACK),
+                in_=wd_raw[:, :, cols].rearrange("p j (c i) -> p c j i", i=4),
+            )
+            nc.vector.quantize_mx(out=wd_codes[:, cols].bitcast(FP8X4), scales=wd_scale[:, cols], in_=wd_bf[:])
+            for c in range(2 * h, 2 * h + 2):
+                feats = slice(c * P, (c + 1) * P)
+                y = y_psum.tile([P, T], F32, name="y")
+                for tokens in (slice(0, 256), slice(256, 384)):
+                    nc.tensor.matmul_mx(
+                        out=y[:, tokens],
+                        lhsT=wd_codes[:, feats].bitcast(FP8X4),
+                        lhsT_scale=wd_scale[:, feats],
+                        rhs=hid_codes[:, tokens].bitcast(FP8X4),
+                        rhs_scale=hid_scale[:, tokens],
+                        start=True,
+                        stop=True,
+                    )
+                early = keep.tile([P, T - P], F32, name=f"early{c}")
+                nc.scalar.copy(out=early[:], in_=y[:, 0 : T - P])
+                nc.sync.dma_start(out=out[feats, 0 : T - P], in_=early[:])
+        for h in range(2):
+            y = y_psum.tile([P, 2, P], F32, name="y")
+            for c in range(2):
+                feats = slice((2 * h + c) * P, (2 * h + c + 1) * P)
+                nc.tensor.matmul_mx(
+                    out=y[:, c, :],
+                    lhsT=wd_codes[:, feats].bitcast(FP8X4),
+                    lhsT_scale=wd_scale[:, feats],
+                    rhs=hid_codes[:, last].bitcast(FP8X4),
+                    rhs_scale=hid_scale[:, last],
+                    start=True,
+                    stop=True,
+                )
+            late = keep.tile([P, 2, P], F32, name=f"late{h}")
+            target = out[h * 256 : (h + 1) * 256, last].rearrange("(c p) t -> p c t", p=P)
+            if h == 0:
+                nc.vector.tensor_copy(out=late[:], in_=y[:])
+                nc.sync.dma_start(out=target, in_=late[:])
+            else:
+                nc.scalar.copy(out=late[:], in_=y[:])
+                nc.scalar.dma_start(out=target, in_=late[:])

@@ -36,10 +36,8 @@ def tile_list_outlier_channels_mlp_kernel(
     nc = tc.nc
     with ExitStack() as ctx:
         keep = ctx.enter_context(tc.tile_pool(name="keep", bufs=1))
-        work = ctx.enter_context(tc.tile_pool(name="work", bufs=2))
-        z_psum = ctx.enter_context(tc.psum_pool(name="z_psum", bufs=2))
-        turn_psum = ctx.enter_context(tc.psum_pool(name="turn_psum", bufs=2))
-        y_psum = ctx.enter_context(tc.psum_pool(name="y_psum", bufs=4))
+        shared = ctx.enter_context(tc.tile_pool(name="shared", bufs=1))
+        psum = ctx.enter_context(tc.psum_pool(name="psum", bufs=1))
 
         offsets = keep.tile([P, J // 16], U16, name="offsets")
         wb_scale_raw = keep.tile([P, PASSES, R], U8, align_bytes=64)
@@ -54,41 +52,127 @@ def tile_list_outlier_channels_mlp_kernel(
         nc.vector.memset(wb_scale[:].bitcast(I32), 0)
 
         for q in range(4):
-            nc.scalar.dma_start(
+            nc.sync.dma_start(
                 out=wb_scale_raw[32 * q : 32 * q + 4, :, :].bitcast(I32),
                 in_=wb_scales[:, 4 * q : 4 * q + 4, :].rearrange("z r c -> r z c").bitcast(I32),
             )
-        load_scale_rows(nc.scalar, xb_scale, xb_scales)
-        load_scale_rows(nc.gpsimd, wo_scale_raw, wo_scales)
-
         wb_raw = keep.tile([P, PASSES, 2 * R], U8, align_bytes=64)
         xb = keep.tile([P, PASSES, 2 * T], U8, align_bytes=64)
         wo_raw = keep.tile([P, R], I32, align_bytes=64)
         nc.sync.dma_start(out=wb_raw[:].bitcast(I32), in_=wb_words.rearrange("z p c -> p z c").bitcast(I32))
         nc.sync.dma_start(out=xb[:].bitcast(I32), in_=xb_words.rearrange("z p c -> p z c").bitcast(I32))
+        load_scale_rows(nc.sync, xb_scale, xb_scales)
         nc.sync.dma_start(offsets[:], offs)
+        row_bytes = 4 * K
+        half_bytes = 4 * PACK * (N // 2)
+        rows = [shared.tile([P, K], F32, name=f"rows{i}", offset=i * row_bytes, align_bytes=64) for i in range(TILES)]
+        nc.sync.dma_start(out=rows[0][:], in_=xt[0:P, :])
         nc.sync.dma_start(out=wo_raw[:], in_=wo_words[0].rearrange("p c t -> p (c t)").bitcast(I32))
-        rows = [keep.tile([P, K], F32, name=f"rows{i}") for i in range(TILES)]
-        for i in range(TILES):
+        load_scale_rows(nc.sync, wo_scale_raw, wo_scales)
+        for i in range(1, TILES):
             nc.sync.dma_start(out=rows[i][:], in_=xt[i * P : (i + 1) * P, :])
-        wd_raw = keep.tile([P, PACK, N], F32)
-        wd_rows = wd.rearrange("(m j e) n -> e m j n", j=PACK, e=4)
-        for e in range(4):
-            nc.sync.dma_start(out=wd_raw[e:P:4, :, :], in_=wd_rows[e])
+        wd_at = [TILES * row_bytes + h * half_bytes for h in range(2)]
+        wd_raw = [shared.tile([P, PACK, N // 2], F32, name=f"wd_raw{h}", offset=wd_at[h], align_bytes=64) for h in range(2)]
+        wd_rows = wd.rearrange("(m j e) (h n) -> h e m j n", j=PACK, e=4, h=2)
+        for h in range(2):
+            for e in range(4):
+                nc.sync.dma_start(out=wd_raw[h][e:P:4, :, :], in_=wd_rows[h, e])
 
         wb = keep.tile([P, PASSES, PACK, 2 * P], U8, align_bytes=64)
-        wo = keep.tile([P, PACK, P], I32, align_bytes=64)
-        wo_scale = keep.tile([P, PACK, P], U8, align_bytes=64)
-        nc.vector.tensor_copy(
-            out=wb[:].bitcast(I32).rearrange("p z j (m w) -> p z j m w", w=2),
-            in_=wb_raw[:].bitcast(I32).rearrange("p z (m j w) -> p z j m w", j=PACK, w=2),
-        )
         for q in range(4):
             live = slice(32 * q, 32 * q + 4)
             nc.vector.tensor_copy(
                 out=wb_scale[live].bitcast(I32),
                 in_=wb_scale_raw[live].bitcast(I32).rearrange("p z (m j) -> p z j m", j=PACK),
             )
+        nc.vector.tensor_copy(
+            out=wb[:].bitcast(I32).rearrange("p z j (m w) -> p z j m w", w=2),
+            in_=wb_raw[:].bitcast(I32).rearrange("p z (m j w) -> p z j m w", j=PACK, w=2),
+        )
+
+        picked = [keep.tile([P, J], BF16, name=f"picked{i}", align_bytes=64) for i in range(TILES)]
+        xo = [keep.tile([P, P * PACK], BF16, name=f"xo{i}", align_bytes=64) for i in range(TILES)]
+        hid = [keep.tile([P, P * PACK], BF16, name=f"hid{i}", align_bytes=64) for i in range(TILES)]
+        wd_bf = [keep.tile([P, 256 * PACK], BF16, name=f"wd_bf{h}", align_bytes=64) for h in range(2)]
+        xo_at = [row_bytes, 2 * row_bytes, 3 * row_bytes, wd_at[0] + 2048]
+        hid_at = [2 * row_bytes + 1024, 3 * row_bytes + 1024, wd_at[0] + 1024, wd_at[1]]
+        xo_codes = [shared.tile([P, P], U32, name=f"xo_codes{i}", offset=xo_at[i], align_bytes=64) for i in range(TILES)]
+        hid_codes = [shared.tile([P, P], U32, name=f"hid_codes{i}", offset=hid_at[i], align_bytes=64) for i in range(TILES)]
+        xo_scale = [keep.tile([P, P], U8, name=f"xo_scale{i}", align_bytes=64) for i in range(TILES)]
+        hid_scale = [keep.tile([P, P], U8, name=f"hid_scale{i}", align_bytes=64) for i in range(TILES)]
+        wd_codes = keep.tile([P, N], U32, align_bytes=64)
+        wd_scale = keep.tile([P, N], U8, align_bytes=64)
+
+        def gather(i):
+            nc.vector.tensor_copy(out=picked[i][:], in_=rows[i][:].indirect(offsets[:]))
+
+        def turn(i):
+            turned = psum.tile([P, 2, P], F32, name=f"turned{i}", tag=f"bank{i + 2}")
+            pairs = picked[i][:].bitcast(F32)
+            for u in range(2):
+                nc.tensor.transpose(turned[:, u, :], pairs[:, u : J // 2 : 2], identity[:])
+            nc.scalar.copy(
+                out=xo[i][:].bitcast(F32).rearrange("p (t u) -> p t u", u=2),
+                in_=turned[:].rearrange("p u t -> p t u"),
+            )
+
+        def quantize(codes, scale, values):
+            nc.vector.quantize_mx(out=codes.bitcast(FP8X4), scales=scale, in_=values)
+
+        def round_wd(h):
+            nc.vector.tensor_copy(
+                out=wd_bf[h][:].rearrange("p (c i j) -> p c j i", i=4, j=PACK),
+                in_=wd_raw[h][:].rearrange("p j (c i) -> p c j i", i=4),
+            )
+
+        def quantize_wd(h):
+            cols = slice(h * 256, (h + 1) * 256)
+            quantize(wd_codes[:, cols], wd_scale[:, cols], wd_bf[h][:])
+
+        def first_layer(i):
+            z = psum.tile([P, PACK, P], F32, name=f"z{i}", tag=f"bank{i}")
+            for j in range(PACK):
+                for g in range(PASSES):
+                    nc.tensor.matmul_mx(
+                        out=z[:, j, :],
+                        lhsT=wb[:, g, j, :].bitcast(FP4X4),
+                        lhsT_scale=wb_scale[:, g, j, :],
+                        rhs=xb[:, g, 2 * i * P : 2 * (i + 1) * P].bitcast(FP4X4),
+                        rhs_scale=xb_scale[:, g, i * P : (i + 1) * P],
+                        start=(j == 0 and g == 0),
+                        stop=False,
+                    )
+            for j in range(PACK):
+                nc.tensor.matmul_mx(
+                    out=z[:, j, :],
+                    lhsT=wo[:, j, :].bitcast(FP8X4),
+                    lhsT_scale=wo_scale[:, j, :],
+                    rhs=xo_codes[i][:].bitcast(FP8X4),
+                    rhs_scale=xo_scale[i][:],
+                    start=False,
+                    stop=(j == PACK - 1),
+                )
+            nc.scalar.activation(
+                out=hid[i][:].rearrange("p (t j) -> p t j", j=PACK),
+                in_=z[:].rearrange("p j t -> p t j"),
+                func=RELU,
+            )
+
+        def second_layer(target, c, i):
+            feats = slice(c * P, (c + 1) * P)
+            nc.tensor.matmul_mx(
+                out=target,
+                lhsT=wd_codes[:, feats].bitcast(FP8X4),
+                lhsT_scale=wd_scale[:, feats],
+                rhs=hid_codes[i][:].bitcast(FP8X4),
+                rhs_scale=hid_scale[i][:],
+                start=True,
+                stop=True,
+            )
+
+        gather(0)
+        wo = shared.tile([P, PACK, P], I32, offset=0, align_bytes=64)
+        wo_scale = shared.tile([P, PACK, P], U8, offset=2048, align_bytes=64)
         nc.vector.tensor_copy(
             out=wo[:].rearrange("p j (m e) -> p j m e", e=4),
             in_=wo_raw[:].rearrange("p (m j e) -> p j m e", j=PACK, e=4),
@@ -97,100 +181,48 @@ def tile_list_outlier_channels_mlp_kernel(
             out=wo_scale[:].bitcast(I32),
             in_=wo_scale_raw[:, 0, :].bitcast(I32).rearrange("p (m j) -> p j m", j=PACK),
         )
-
-        hid_codes = keep.tile([P, T], U32, align_bytes=64)
-        hid_scale = keep.tile([P, T], U8, align_bytes=64)
         for i in range(TILES):
-            tokens = slice(i * P, (i + 1) * P)
-            z = z_psum.tile([P, PACK, P], F32)
-            for j in range(PACK):
-                for g in range(PASSES):
-                    nc.tensor.matmul_mx(
-                        out=z[:, j, :],
-                        lhsT=wb[:, g, j, :].bitcast(FP4X4),
-                        lhsT_scale=wb_scale[:, g, j, :],
-                        rhs=xb[:, g, 2 * i * P : 2 * (i + 1) * P].bitcast(FP4X4),
-                        rhs_scale=xb_scale[:, g, tokens],
-                        start=(j == 0 and g == 0),
-                        stop=False,
-                    )
-            picked = work.tile([P, J], BF16, align_bytes=64)
-            nc.vector.tensor_copy(out=picked[:], in_=rows[i][:].indirect(offsets[:]))
-            turned = turn_psum.tile([P, 2, P], F32)
-            pairs = picked[:].bitcast(F32)
-            for u in range(2):
-                nc.tensor.transpose(turned[:, u, :], pairs[:, u : J // 2 : 2], identity[:])
-            xo = work.tile([P, P * PACK], BF16, align_bytes=64)
-            nc.scalar.copy(
-                out=xo[:].bitcast(F32).rearrange("p (t u) -> p t u", u=2),
-                in_=turned[:].rearrange("p u t -> p t u"),
-            )
-            xo_codes = work.tile([P, P], U32, align_bytes=64)
-            xo_scale = work.tile([P, P], U8, align_bytes=64)
-            nc.vector.quantize_mx(out=xo_codes[:].bitcast(FP8X4), scales=xo_scale[:], in_=xo[:])
-            for j in range(PACK):
-                nc.tensor.matmul_mx(
-                    out=z[:, j, :],
-                    lhsT=wo[:, j, :].bitcast(FP8X4),
-                    lhsT_scale=wo_scale[:, j, :],
-                    rhs=xo_codes[:].bitcast(FP8X4),
-                    rhs_scale=xo_scale[:],
-                    start=False,
-                    stop=(j == PACK - 1),
-                )
-            hid = work.tile([P, P * PACK], BF16, align_bytes=64)
-            nc.scalar.activation(
-                out=hid[:].rearrange("p (t j) -> p t j", j=PACK),
-                in_=z[:].rearrange("p j t -> p t j"),
-                func=RELU,
-            )
-            nc.vector.quantize_mx(out=hid_codes[:, tokens].bitcast(FP8X4), scales=hid_scale[:, tokens], in_=hid[:])
-
-        wd_codes = keep.tile([P, N], U32, align_bytes=64)
-        wd_scale = keep.tile([P, N], U8, align_bytes=64)
-        last = slice(T - P, T)
-        for h in range(2):
-            cols = slice(h * 256, (h + 1) * 256)
-            wd_bf = work.tile([P, 256 * PACK], BF16, align_bytes=64)
-            nc.vector.tensor_copy(
-                out=wd_bf[:].rearrange("p (c i j) -> p c j i", i=4, j=PACK),
-                in_=wd_raw[:, :, cols].rearrange("p j (c i) -> p c j i", i=4),
-            )
-            nc.vector.quantize_mx(out=wd_codes[:, cols].bitcast(FP8X4), scales=wd_scale[:, cols], in_=wd_bf[:])
-            for c in range(2 * h, 2 * h + 2):
-                feats = slice(c * P, (c + 1) * P)
-                y = y_psum.tile([P, T], F32, name="y")
-                for tokens in (slice(0, 256), slice(256, 384)):
-                    nc.tensor.matmul_mx(
-                        out=y[:, tokens],
-                        lhsT=wd_codes[:, feats].bitcast(FP8X4),
-                        lhsT_scale=wd_scale[:, feats],
-                        rhs=hid_codes[:, tokens].bitcast(FP8X4),
-                        rhs_scale=hid_scale[:, tokens],
-                        start=True,
-                        stop=True,
-                    )
-                early = keep.tile([P, T - P], F32, name=f"early{c}")
-                nc.scalar.copy(out=early[:], in_=y[:, 0 : T - P])
-                nc.sync.dma_start(out=out[feats, 0 : T - P], in_=early[:])
-        for h in range(2):
-            y = y_psum.tile([P, 2, P], F32, name="y")
-            for c in range(2):
-                feats = slice((2 * h + c) * P, (2 * h + c + 1) * P)
-                nc.tensor.matmul_mx(
-                    out=y[:, c, :],
-                    lhsT=wd_codes[:, feats].bitcast(FP8X4),
-                    lhsT_scale=wd_scale[:, feats],
-                    rhs=hid_codes[:, last].bitcast(FP8X4),
-                    rhs_scale=hid_scale[:, last],
-                    start=True,
-                    stop=True,
-                )
-            late = keep.tile([P, 2, P], F32, name=f"late{h}")
-            target = out[h * 256 : (h + 1) * 256, last].rearrange("(c p) t -> p c t", p=P)
-            if h == 0:
-                nc.vector.tensor_copy(out=late[:], in_=y[:])
-                nc.sync.dma_start(out=target, in_=late[:])
+            turn(i)
+            if i + 1 < TILES:
+                gather(i + 1)
             else:
-                nc.scalar.copy(out=late[:], in_=y[:])
-                nc.scalar.dma_start(out=target, in_=late[:])
+                round_wd(0)
+            quantize(xo_codes[i][:], xo_scale[i][:], xo[i][:])
+            if i + 1 == TILES:
+                quantize_wd(0)
+            if i > 0:
+                quantize(hid_codes[i - 1][:], hid_scale[i - 1][:], hid[i - 1][:])
+            first_layer(i)
+        round_wd(1)
+        last = TILES - 1
+        quantize(hid_codes[last][:], hid_scale[last][:], hid[last][:])
+        quantize_wd(1)
+
+        early = [
+            shared.tile([P, last, P], F32, name="early0", offset=xo_at[last], align_bytes=64),
+            keep.tile([P, last, P], F32, name="early1"),
+        ]
+        for c in range(2):
+            y = psum.tile([P, last, P], F32, name=f"y{c}", tag=f"bank{6 + c}")
+            for i in range(last):
+                second_layer(y[:, i, :], c, i)
+            nc.scalar.copy(out=early[c][:], in_=y[:])
+            nc.sync.dma_start(out=out[c * P : (c + 1) * P, 0 : last * P], in_=early[c][:].rearrange("p i t -> p (i t)"))
+        y = psum.tile([P, 2, P], F32, name="y_late", tag="bank4")
+        for c in range(2):
+            second_layer(y[:, c, :], c, last)
+        late = keep.tile([P, 2, P], F32)
+        nc.scalar.copy(out=late[:], in_=y[:])
+        nc.sync.dma_start(out=out[0:256, last * P : T].rearrange("(c p) t -> p c t", p=P), in_=late[:])
+        for c in range(2, 4):
+            y = psum.tile([P, TILES, P], F32, name=f"y{c}", tag=f"bank{c - 2}")
+            for i in range(TILES):
+                second_layer(y[:, i, :], c, i)
+            whole = keep.tile([P, TILES, P], F32, name=f"whole{c}")
+            target = out[c * P : (c + 1) * P, :]
+            if c == 2:
+                nc.vector.tensor_copy(out=whole[:], in_=y[:])
+                nc.sync.dma_start(out=target, in_=whole[:].rearrange("p i t -> p (i t)"))
+            else:
+                nc.scalar.copy(out=whole[:], in_=y[:])
+                nc.scalar.dma_start(out=target, in_=whole[:].rearrange("p i t -> p (i t)"))

from contextlib import ExitStack

import concourse.mybir as mybir
from concourse.masks import make_identity

K, J, T, R, N = 2048, 512, 512, 512, 512
FLOPS = 2 * T * R * (K + J) + 2 * T * R * N

F32 = mybir.dt.float32
BF16 = mybir.dt.bfloat16
I32 = mybir.dt.int32
U32 = mybir.dt.uint32
U16 = mybir.dt.uint16
U8 = mybir.dt.uint8
FP8X4 = mybir.dt.float8_e4m3fn_x4
FP4X4 = mybir.dt.float4_e2m1fn_x4
RELU = mybir.ActivationFunctionType.Relu

P = 128
PACK = 4
PASSES = K // (P * PACK)
TILES = T // P


def load_scale_rows(queue, plane, scales):
    for r in range(4):
        queue.dma_start(
            out=plane[r:P:32, :, :].bitcast(I32),
            in_=scales[:, r:16:4, :].rearrange("z q c -> q z c").bitcast(I32),
        )


def tile_list_outlier_channels_mlp_kernel(
    tc, xb_words, xb_scales, wb_words, wb_scales, xt, wo_words, wo_scales, wd, offs, out
):
    nc = tc.nc
    with ExitStack() as ctx:
        keep = ctx.enter_context(tc.tile_pool(name="keep", bufs=1))
        shared = ctx.enter_context(tc.tile_pool(name="shared", bufs=1))
        psum = ctx.enter_context(tc.psum_pool(name="psum", bufs=1))

        offsets = keep.tile([P, J // 16], U16, name="offsets")
        wb_scale_raw = keep.tile([P, PASSES, R], U8, align_bytes=64)
        wb_scale = keep.tile([P, PASSES, PACK, P], U8, align_bytes=64)
        xb_scale = keep.tile([P, PASSES, T], U8, align_bytes=64)
        wo_scale_raw = keep.tile([P, 1, R], U8, align_bytes=64)
        nc.gpsimd.memset(xb_scale[:].bitcast(I32), 0)
        nc.vector.memset(wo_scale_raw[:].bitcast(I32), 0)
        identity = keep.tile([P, P], F32)
        nc.vector.memset(identity[:], 0.0)
        make_identity(nc, identity[:], nomemset=True)
        nc.vector.memset(wb_scale[:].bitcast(I32), 0)

        for q in range(4):
            nc.sync.dma_start(
                out=wb_scale_raw[32 * q : 32 * q + 4, :, :].bitcast(I32),
                in_=wb_scales[:, 4 * q : 4 * q + 4, :].rearrange("z r c -> r z c").bitcast(I32),
            )
        wb_raw = keep.tile([P, PASSES, 2 * R], U8, align_bytes=64)
        xb = keep.tile([P, PASSES, 2 * T], U8, align_bytes=64)
        wo_raw = keep.tile([P, R], I32, align_bytes=64)
        nc.sync.dma_start(out=wb_raw[:].bitcast(I32), in_=wb_words.rearrange("z p c -> p z c").bitcast(I32))
        nc.sync.dma_start(out=xb[:].bitcast(I32), in_=xb_words.rearrange("z p c -> p z c").bitcast(I32))
        load_scale_rows(nc.sync, xb_scale, xb_scales)
        nc.sync.dma_start(offsets[:], offs)
        row_bytes = 4 * K
        half_bytes = 4 * PACK * (N // 2)
        rows = [shared.tile([P, K], F32, name=f"rows{i}", offset=i * row_bytes, align_bytes=64) for i in range(TILES)]
        nc.sync.dma_start(out=rows[0][:], in_=xt[0:P, :])
        nc.sync.dma_start(out=wo_raw[:], in_=wo_words[0].rearrange("p c t -> p (c t)").bitcast(I32))
        load_scale_rows(nc.sync, wo_scale_raw, wo_scales)
        for i in range(1, TILES):
            nc.sync.dma_start(out=rows[i][:], in_=xt[i * P : (i + 1) * P, :])
        wd_at = [TILES * row_bytes + h * half_bytes for h in range(2)]
        wd_raw = [shared.tile([P, PACK, N // 2], F32, name=f"wd_raw{h}", offset=wd_at[h], align_bytes=64) for h in range(2)]
        wd_rows = wd.rearrange("(m j e) (h n) -> h e m j n", j=PACK, e=4, h=2)
        for h in range(2):
            for e in range(4):
                nc.sync.dma_start(out=wd_raw[h][e:P:4, :, :], in_=wd_rows[h, e])

        wb = keep.tile([P, PASSES, PACK, 2 * P], U8, align_bytes=64)
        for q in range(4):
            live = slice(32 * q, 32 * q + 4)
            nc.vector.tensor_copy(
                out=wb_scale[live].bitcast(I32),
                in_=wb_scale_raw[live].bitcast(I32).rearrange("p z (m j) -> p z j m", j=PACK),
            )
        nc.vector.tensor_copy(
            out=wb[:].bitcast(I32).rearrange("p z j (m w) -> p z j m w", w=2),
            in_=wb_raw[:].bitcast(I32).rearrange("p z (m j w) -> p z j m w", j=PACK, w=2),
        )

        picked = [keep.tile([P, J], BF16, name=f"picked{i}", align_bytes=64) for i in range(TILES)]
        xo = [keep.tile([P, P * PACK], BF16, name=f"xo{i}", align_bytes=64) for i in range(TILES)]
        hid = [keep.tile([P, P * PACK], BF16, name=f"hid{i}", align_bytes=64) for i in range(TILES)]
        wd_bf = [keep.tile([P, 256 * PACK], BF16, name=f"wd_bf{h}", align_bytes=64) for h in range(2)]
        xo_at = [row_bytes, 2 * row_bytes, 3 * row_bytes, wd_at[0] + 2048]
        hid_at = [2 * row_bytes + 1024, 3 * row_bytes + 1024, wd_at[0] + 1024, wd_at[1]]
        xo_codes = [shared.tile([P, P], U32, name=f"xo_codes{i}", offset=xo_at[i], align_bytes=64) for i in range(TILES)]
        hid_codes = [shared.tile([P, P], U32, name=f"hid_codes{i}", offset=hid_at[i], align_bytes=64) for i in range(TILES)]
        xo_scale = [keep.tile([P, P], U8, name=f"xo_scale{i}", align_bytes=64) for i in range(TILES)]
        hid_scale = [keep.tile([P, P], U8, name=f"hid_scale{i}", align_bytes=64) for i in range(TILES)]
        wd_codes = keep.tile([P, N], U32, align_bytes=64)
        wd_scale = keep.tile([P, N], U8, align_bytes=64)

        def gather(i):
            nc.vector.tensor_copy(out=picked[i][:], in_=rows[i][:].indirect(offsets[:]))

        def turn(i):
            turned = psum.tile([P, 2, P], F32, name=f"turned{i}", tag=f"bank{i + 2}")
            pairs = picked[i][:].bitcast(F32)
            for u in range(2):
                nc.tensor.transpose(turned[:, u, :], pairs[:, u : J // 2 : 2], identity[:])
            nc.scalar.copy(
                out=xo[i][:].bitcast(F32).rearrange("p (t u) -> p t u", u=2),
                in_=turned[:].rearrange("p u t -> p t u"),
            )

        def quantize(codes, scale, values):
            nc.vector.quantize_mx(out=codes.bitcast(FP8X4), scales=scale, in_=values)

        def round_wd(h):
            nc.vector.tensor_copy(
                out=wd_bf[h][:].rearrange("p (c i j) -> p c j i", i=4, j=PACK),
                in_=wd_raw[h][:].rearrange("p j (c i) -> p c j i", i=4),
            )

        def quantize_wd(h):
            cols = slice(h * 256, (h + 1) * 256)
            quantize(wd_codes[:, cols], wd_scale[:, cols], wd_bf[h][:])

        def first_layer(i):
            z = psum.tile([P, PACK, P], F32, name=f"z{i}", tag=f"bank{i}")
            for j in range(PACK):
                for g in range(PASSES):
                    nc.tensor.matmul_mx(
                        out=z[:, j, :],
                        lhsT=wb[:, g, j, :].bitcast(FP4X4),
                        lhsT_scale=wb_scale[:, g, j, :],
                        rhs=xb[:, g, 2 * i * P : 2 * (i + 1) * P].bitcast(FP4X4),
                        rhs_scale=xb_scale[:, g, i * P : (i + 1) * P],
                        start=(j == 0 and g == 0),
                        stop=False,
                    )
            for j in range(PACK):
                nc.tensor.matmul_mx(
                    out=z[:, j, :],
                    lhsT=wo[:, j, :].bitcast(FP8X4),
                    lhsT_scale=wo_scale[:, j, :],
                    rhs=xo_codes[i][:].bitcast(FP8X4),
                    rhs_scale=xo_scale[i][:],
                    start=False,
                    stop=(j == PACK - 1),
                )
            nc.scalar.activation(
                out=hid[i][:].rearrange("p (t j) -> p t j", j=PACK),
                in_=z[:].rearrange("p j t -> p t j"),
                func=RELU,
            )

        def second_layer(target, c, i):
            feats = slice(c * P, (c + 1) * P)
            nc.tensor.matmul_mx(
                out=target,
                lhsT=wd_codes[:, feats].bitcast(FP8X4),
                lhsT_scale=wd_scale[:, feats],
                rhs=hid_codes[i][:].bitcast(FP8X4),
                rhs_scale=hid_scale[i][:],
                start=True,
                stop=True,
            )

        gather(0)
        wo = shared.tile([P, PACK, P], I32, offset=0, align_bytes=64)
        wo_scale = shared.tile([P, PACK, P], U8, offset=2048, align_bytes=64)
        nc.vector.tensor_copy(
            out=wo[:].rearrange("p j (m e) -> p j m e", e=4),
            in_=wo_raw[:].rearrange("p (m j e) -> p j m e", j=PACK, e=4),
        )
        nc.vector.tensor_copy(
            out=wo_scale[:].bitcast(I32),
            in_=wo_scale_raw[:, 0, :].bitcast(I32).rearrange("p (m j) -> p j m", j=PACK),
        )
        for i in range(TILES):
            turn(i)
            if i + 1 < TILES:
                gather(i + 1)
            else:
                round_wd(0)
            quantize(xo_codes[i][:], xo_scale[i][:], xo[i][:])
            if i + 1 == TILES:
                quantize_wd(0)
            if i > 0:
                quantize(hid_codes[i - 1][:], hid_scale[i - 1][:], hid[i - 1][:])
            first_layer(i)
        round_wd(1)
        last = TILES - 1
        quantize(hid_codes[last][:], hid_scale[last][:], hid[last][:])
        quantize_wd(1)

        early = [
            shared.tile([P, last, P], F32, name="early0", offset=xo_at[last], align_bytes=64),
            keep.tile([P, last, P], F32, name="early1"),
        ]
        for c in range(2):
            y = psum.tile([P, last, P], F32, name=f"y{c}", tag=f"bank{6 + c}")
            for i in range(last):
                second_layer(y[:, i, :], c, i)
            nc.scalar.copy(out=early[c][:], in_=y[:])
            nc.sync.dma_start(out=out[c * P : (c + 1) * P, 0 : last * P], in_=early[c][:].rearrange("p i t -> p (i t)"))
        y = psum.tile([P, 2, P], F32, name="y_late", tag="bank4")
        for c in range(2):
            second_layer(y[:, c, :], c, last)
        late = keep.tile([P, 2, P], F32)
        nc.scalar.copy(out=late[:], in_=y[:])
        nc.sync.dma_start(out=out[0:256, last * P : T].rearrange("(c p) t -> p c t", p=P), in_=late[:])
        for c in range(2, 4):
            y = psum.tile([P, TILES, P], F32, name=f"y{c}", tag=f"bank{c - 2}")
            for i in range(TILES):
                second_layer(y[:, i, :], c, i)
            whole = keep.tile([P, TILES, P], F32, name=f"whole{c}")
            target = out[c * P : (c + 1) * P, :]
            if c == 2:
                nc.vector.tensor_copy(out=whole[:], in_=y[:])
                nc.sync.dma_start(out=target, in_=whole[:].rearrange("p i t -> p (i t)"))
            else:
                nc.scalar.copy(out=whole[:], in_=y[:])
                nc.scalar.dma_start(out=target, in_=whole[:].rearrange("p i t -> p (i t)"))
